import numpy as np
import ml_dtypes


def mxq(x, axis, fmt="e4m3"):
    dtype, down = {"e4m3": (ml_dtypes.float8_e4m3fn, 7), "e5m2": (ml_dtypes.float8_e5m2, 14)}[fmt]
    v = np.moveaxis(np.asarray(x, np.float32).astype(ml_dtypes.bfloat16).astype(np.float64), axis, -1)
    blocks = v.reshape(v.shape[:-1] + (-1, 32))
    amax = np.abs(blocks).max(-1, keepdims=True)
    byte = np.maximum(np.where(amax > 0, np.frexp(amax)[1] - 1 + 127, 0) - down, 1)
    scale = np.exp2(byte - 127.0)
    codes = (blocks / scale).astype(np.float32).astype(dtype).astype(np.float64)
    return np.moveaxis((codes * scale).reshape(v.shape), -1, axis)


WIDE = False


def mx_kscale(k):
    if not WIDE:
        return np.ones(k)
    levels = np.array([30, -30])
    if k % 512:
        return np.exp2(np.random.permutation(np.resize(levels, k // 32))).repeat(32)
    a = np.empty((k // 512, 16))
    for p in range(k // 512):
        a[p, :8] = np.random.permutation(np.resize(levels, 8))
        for g in range(8):
            far = levels[np.abs(levels - a[p, g]) >= 10]
            a[p, g + 8] = far[np.random.randint(len(far))]
    return np.exp2(a.ravel()).repeat(32)


def f64(x):
    return np.asarray(x).astype(np.float64)


def striped(idx):
    return np.tile(np.asarray(idx).reshape(-1, 16).T, (8, 1)).astype(np.uint16)


def unstriped(offs):
    return offs[:16].T.reshape(-1).astype(np.int64)


E2M1 = np.array([0.0, 0.5, 1.0, 1.5, 2.0, 3.0, 4.0, 6.0, -0.0, -0.5, -1.0, -1.5, -2.0, -3.0, -4.0, -6.0])


def pack_weight(w, fmt):
    k, n = w.shape
    w = f64(np.asarray(w, np.float32).astype(ml_dtypes.bfloat16)).reshape(k // 32, 32, n)
    amax = np.abs(w).max(1)
    if fmt == "e4m3":
        byte = np.frexp(amax)[1] - 1 + 127 - 7
    else:
        mant, ex = np.frexp(amax / 6.0)
        byte = np.where(mant > 0.5, ex, ex - 1) + 127
    byte = np.clip(np.where(amax > 0, byte, 1), 1, 254)
    scaled = (w * np.exp2(127.0 - byte)[:, None, :]).reshape(k, n).astype(np.float32)
    by_word = np.ascontiguousarray(scaled.reshape(k // 512, 128, 4, n).transpose(0, 1, 3, 2))
    if fmt == "e4m3":
        words = by_word.astype(ml_dtypes.float8_e4m3fn).view(np.uint8)
    else:
        c = by_word.astype(ml_dtypes.float4_e2m1fn).view(np.uint8) & 0xF
        words = (c[..., 0::2] | (c[..., 1::2] << 4)).reshape(k // 512, 128, 2 * n)
    return np.ascontiguousarray(words), np.ascontiguousarray(byte.astype(np.uint8).reshape(k // 512, 16, n))


def unpack_weight(words, scales, fmt):
    g, _, n = scales.shape
    words = np.ascontiguousarray(words).reshape(g, 128, n, -1)
    if fmt == "e4m3":
        vals = words.view(ml_dtypes.float8_e4m3fn).astype(np.float64)
    else:
        nib = np.empty((g, 128, n, 4), np.uint8)
        nib[..., 0::2] = words & 0xF
        nib[..., 1::2] = words >> 4
        vals = E2M1[nib]
    vals = vals * np.repeat(np.exp2(scales.astype(np.float64) - 127.0), 8, axis=1)[..., None]
    return vals.transpose(0, 1, 3, 2).reshape(g * 512, n)


def bf(x):
    return np.asarray(x, np.float32).astype(ml_dtypes.bfloat16)


def planes(Y):
    r, m = Y.shape
    b = f64(bf(Y)).reshape(r // 32, 32, m)
    amax = np.abs(b).max(1)
    byte = np.clip(np.where(amax > 0, np.frexp(amax)[1] - 1 + 127 - 7, 1), 1, 254)
    codes = (b * np.exp2(127.0 - byte)[:, None, :]).reshape(r, m).astype(np.float32).astype(ml_dtypes.float8_e4m3fn).view(np.uint8)
    words = codes.reshape(r // 512, 128, 4, m).transpose(0, 1, 3, 2)
    return np.ascontiguousarray(words), np.ascontiguousarray(byte.astype(np.uint8).reshape(r // 512, 16, m))


K, N, T, J = 512, 512, 1024, 512


def setup_inputs():
    n = np.random.standard_normal
    idx = np.random.permutation(T)[:J]
    fk = mx_kscale(K)
    fn = mx_kscale(N)
    xtp = pack_weight(n((K, T)) / fk[:, None], "e2m1")
    wnp = pack_weight(n((K, N)) * 1 / np.sqrt(K) * fk[:, None], "e4m3")
    wtp = pack_weight(n((N, K)) * 1 / np.sqrt(N) / fn[:, None], "e2m1")
    return {
        "xt_words": xtp[0],
        "xt_scales": xtp[1],
        "wn_words": wnp[0],
        "wn_scales": wnp[1],
        "te": (n((N, T))).astype(np.float32),
        "us": (np.random.uniform(0.5, 2.0, (N, 1)) * fn[:, None]).astype(np.float32),
        "wt_words": wtp[0],
        "wt_scales": wtp[1],
        "run": (0.3 * n((K, T))).astype(np.float32),
        "offs": striped(idx),
    }


def reference(xt_words, xt_scales, wn_words, wn_scales, te, us, wt_words, wt_scales, run, offs):
    idx = unstriped(offs)
    xtu = unpack_weight(xt_words, xt_scales, "e2m1")
    wnu = unpack_weight(wn_words, wn_scales, "e4m3")
    wtu = unpack_weight(wt_words, wt_scales, "e2m1")
    xtidxg = xtu[:, idx]
    p = wnu.T @ xtidxg
    d = (p - f64(te)[:, idx]) * f64(us)
    dq = mxq(d, 0, "e5m2")
    q = wtu.T @ dq
    qp = np.zeros((K, T))
    qp[:, idx] = q
    y = qp + f64(run)
    words, scales = planes(y)
    return y, words, scales

@@ -1,0 +1,200 @@
+from contextlib import ExitStack
+
+import concourse.mybir as mybir
+
+K, N, T, J = 512, 512, 1024, 512
+FLOPS = 2 * K * N * J * 2
+
+F32 = mybir.dt.float32
+BF16 = mybir.dt.bfloat16
+I32 = mybir.dt.int32
+U16 = mybir.dt.uint16
+U8 = mybir.dt.uint8
+E4M3 = mybir.dt.float8_e4m3fn_x4
+E5M2 = mybir.dt.float8_e5m2_x4
+E2M1 = mybir.dt.float4_e2m1fn_x4
+COPY = mybir.ActivationFunctionType.Copy
+ADD = mybir.AluOpType.add
+SUBTRACT = mybir.AluOpType.subtract
+
+P = 128
+PACK = 4
+HALF = J // 2
+COLS = T // 2
+
+
+def load_scale_plane(nc, plane, scales):
+    words = scales[0].bitcast(I32)
+    for q in range(4):
+        nc.sync.dma_start(out=plane[32 * q : 32 * q + 4, :].bitcast(I32), in_=words[4 * q : 4 * q + 4, :])
+
+
+def tile_moe_expert_taught_by_page_pl_kernel(
+    tc, xt_words, xt_scales, wn_words, wn_scales, te, us, wt_words, wt_scales, run, offs, out_0, out_1, out_2
+):
+    nc = tc.nc
+    with ExitStack() as ctx:
+        keep = ctx.enter_context(tc.tile_pool(name="keep", bufs=1))
+        psum = ctx.enter_context(tc.psum_pool(name="psum", bufs=1))
+
+        def sb(name, shape, dtype):
+            return keep.tile(shape, dtype, name=name, align_bytes=64)
+
+        offsets = keep.tile([P, J // 16], U16, name="offsets")
+        nc.sync.dma_start(offsets[:], offs)
+        half_offsets = [offsets[:, h * (HALF // 16) : (h + 1) * (HALF // 16)] for h in range(2)]
+
+        wn_w = sb("wn_w", [P, 4 * N], U8)
+        wn_s = sb("wn_s", [P, N], U8)
+        xt_w = sb("xt_w", [P, 2 * T], U8)
+        xt_s = sb("xt_s", [P, T], U8)
+        wt_w = sb("wt_w", [P, 2 * K], U8)
+        wt_s = sb("wt_s", [P, K], U8)
+        for plane in (wn_s, xt_s, wt_s):
+            nc.vector.memset(plane[:].bitcast(I32), 0)
+        nc.sync.dma_start(out=xt_w[:].bitcast(I32), in_=xt_words[0].bitcast(I32))
+        nc.sync.dma_start(out=wn_w[:].bitcast(I32), in_=wn_words[0].rearrange("p n t -> p (n t)").bitcast(I32))
+        load_scale_plane(nc, wn_s, wn_scales)
+        load_scale_plane(nc, xt_s, xt_scales)
+
+        te_rows = te.rearrange("(p t) c -> p t c", t=PACK)
+        run_rows = run.rearrange("(p t) c -> p t c", t=PACK)
+        y_rows = out_0.rearrange("(p t) c -> p t c", t=PACK)
+        te_sb = [sb("te%d" % t, [P, T], F32) for t in range(PACK)]
+        for t in range(PACK):
+            nc.sync.dma_start(out=te_sb[t][:], in_=te_rows[:, t, :])
+        us_sb = sb("us_sb", [P, PACK], F32)
+        nc.sync.dma_start(out=us_sb[:], in_=us.rearrange("(p t) o -> p (t o)", t=PACK))
+        nc.sync.dma_start(out=wt_w[:].bitcast(I32), in_=wt_words[0].bitcast(I32))
+        load_scale_plane(nc, wt_s, wt_scales)
+        run_sb = [sb("run%d" % t, [P, T], F32) for t in range(PACK)]
+        for t in range(PACK):
+            nc.sync.dma_start(out=run_sb[t][:], in_=run_rows[:, t, :])
+
+        pages = [sb("page%d" % t, [P, T], F32) for t in range(PACK)]
+        for t in range(PACK):
+            nc.vector.memset(pages[t][:], 0.0)
+
+        neg_us = sb("neg_us", [P, PACK], F32)
+        nc.scalar.activation(out=neg_us[:], in_=us_sb[:], func=COPY, scale=-1.0)
+
+        xg_w = [sb("xg_w%d" % h, [P, 2 * HALF], U8) for h in range(2)]
+        xg_s = [sb("xg_s%d" % h, [P, HALF], U8) for h in range(2)]
+        wn_wp = sb("wn_wp", [P, 4 * N], U8)
+        wn_sp = sb("wn_sp", [P, N], U8)
+
+        for h in range(2):
+            nc.vector.tensor_copy(out=xg_w[h][:].bitcast(U16), in_=xt_w[:].bitcast(U16).indirect(half_offsets[h]))
+        nc.vector.tensor_copy(
+            out=wn_wp[:].bitcast(I32).rearrange("p (t c i) -> p c t i", t=PACK, i=4),
+            in_=wn_w[:].bitcast(I32).rearrange("p (c i t) -> p c t i", t=PACK, i=4),
+        )
+        nc.vector.tensor_copy(
+            out=wn_sp[:].rearrange("p (t m) -> p t m", t=PACK), in_=wn_s[:].rearrange("p (m t) -> p t m", t=PACK)
+        )
+        for h in range(2):
+            nc.vector.tensor_copy(out=xg_s[h][:], in_=xt_s[:].indirect(half_offsets[h]))
+
+        p_sb = {}
+        for h in range(2):
+            for u in range(2):
+                bank = psum.tile([P, 2, HALF], F32, name="p_bank%d%d" % (h, u))
+                for e in range(2):
+                    t = 2 * u + e
+                    nc.tensor.matmul_mx(
+                        out=bank[:, e, :],
+                        lhsT=wn_wp[:, 4 * P * t : 4 * P * (t + 1)].bitcast(E4M3),
+                        lhsT_scale=wn_sp[:, P * t : P * (t + 1)],
+                        rhs=xg_w[h][:].bitcast(E2M1),
+                        rhs_scale=xg_s[h][:],
+                        start=True,
+                        stop=True,
+                    )
+                p_sb[h, u] = sb("p_sb%d%d" % (h, u), [P, 2, HALF], F32)
+                nc.scalar.copy(out=p_sb[h, u][:], in_=bank[:])
+
+        d_codes = sb("d_codes", [P, 4 * J], U8)
+        d_scales = sb("d_scales", [P, J], U8)
+        wt_wp = sb("wt_wp", [P, 2 * K], U8)
+        wt_sp = sb("wt_sp", [P, K], U8)
+        for h in range(2):
+            d_planes = sb("d_planes%d" % h, [P, PACK, HALF], BF16)
+            for t in range(PACK):
+                diff = sb("diff%d%d" % (h, t), [P, HALF], F32)
+                nc.vector.tensor_tensor(
+                    out=diff[:], in0=te_sb[t][:].indirect(half_offsets[h]), in1=p_sb[h, t // 2][:, t % 2, :], op=SUBTRACT
+                )
+                nc.scalar.activation(out=d_planes[:, t, :], in_=diff[:], func=COPY, scale=neg_us[:, t : t + 1])
+            d_grouped = sb("d_grouped%d" % h, [P, HALF, PACK], BF16)
+            dst = d_grouped[:].rearrange("p (c i) t -> p c t i", i=4)
+            src = d_planes[:].rearrange("p t (c i) -> p c t i", i=4)
+            if h == 0:
+                nc.scalar.copy(out=dst, in_=src)
+            else:
+                nc.vector.tensor_copy(
+                    out=wt_wp[:].rearrange("p (t m b) -> p t m b", t=PACK, b=2),
+                    in_=wt_w[:].rearrange("p (m t b) -> p t m b", t=PACK, b=2),
+                )
+                nc.vector.tensor_copy(
+                    out=wt_sp[:].rearrange("p (t m) -> p t m", t=PACK),
+                    in_=wt_s[:].rearrange("p (m t) -> p t m", t=PACK),
+                )
+                nc.vector.tensor_copy(out=dst, in_=src)
+            nc.vector.quantize_mx(
+                out=d_codes[:, 4 * HALF * h : 4 * HALF * (h + 1)].bitcast(E5M2),
+                scales=d_scales[:, HALF * h : HALF * (h + 1)],
+                in_=d_grouped[:].rearrange("p c t -> p (c t)"),
+            )
+
+        y_pairs = {}
+        y_grouped = [sb("y_grouped%d" % g, [P, COLS, PACK], BF16) for g in range(2)]
+        for u in range(2):
+            for g in range(2):
+                y_pairs[u, g] = sb("y_pairs%d%d" % (u, g), [P, 2, COLS], F32)
+        y_codes = sb("y_codes", [P, 4 * T], U8)
+        y_scales = sb("y_scales", [P, T], U8)
+        words_out = out_1[0].rearrange("p c r -> p (c r)").bitcast(I32)
+        scales_out = out_2[0].bitcast(I32)
+
+        for t in range(PACK):
+            bank = psum.tile([P, J], F32, name="q_bank%d" % t)
+            nc.tensor.matmul_mx(
+                out=bank[:],
+                lhsT=wt_wp[:, 2 * P * t : 2 * P * (t + 1)].bitcast(E2M1),
+                lhsT_scale=wt_sp[:, P * t : P * (t + 1)],
+                rhs=d_codes[:].bitcast(E5M2),
+                rhs_scale=d_scales[:],
+                start=True,
+                stop=True,
+            )
+            q_sb = sb("q_sb%d" % t, [P, J], F32)
+            nc.scalar.copy(out=q_sb[:], in_=bank[:])
+            nc.vector.tensor_copy(out=pages[t][:].indirect(offsets[:]), in_=q_sb[:])
+            u, e = divmod(t, 2)
+            last = t == PACK - 1
+            for g in range(2):
+                cols = slice(g * COLS, (g + 1) * COLS)
+                adder = nc.vector if last else nc.gpsimd
+                adder.tensor_tensor(out=y_pairs[u, g][:, e, :], in0=pages[t][:, cols], in1=run_sb[t][:, cols], op=ADD)
+                nc.sync.dma_start(out=y_rows[:, t, cols], in_=y_pairs[u, g][:, e, :])
+            if e == 1:
+                for g in range(2):
+                    dst = y_grouped[g][:, :, 2 * u : 2 * u + 2]
+                    src = y_pairs[u, g][:].rearrange("p e c -> p c e")
+                    if last and g == 1:
+                        nc.vector.tensor_copy(out=dst, in_=src)
+                    else:
+                        nc.scalar.copy(out=dst, in_=src)
+
+        for g in (1, 0):
+            nc.vector.quantize_mx(
+                out=y_codes[:, 4 * COLS * g : 4 * COLS * (g + 1)].bitcast(E4M3),
+                scales=y_scales[:, COLS * g : COLS * (g + 1)],
+                in_=y_grouped[g][:].rearrange("p c t -> p (c t)"),
+            )
+            nc.sync.dma_start(
+                out=words_out[:, COLS * g : COLS * (g + 1)], in_=y_codes[:].bitcast(I32)[:, COLS * g : COLS * (g + 1)]
+            )
+        for q in range(4):
+            queue = nc.sync if q % 2 == 0 else nc.scalar
+            queue.dma_start(out=scales_out[4 * q : 4 * q + 4, :], in_=y_scales[32 * q : 32 * q + 4, :].bitcast(I32))

@@ -1,6 +1,7 @@
 from contextlib import ExitStack
 
 import concourse.mybir as mybir
+from concourse.masks import make_identity
 
 K, N, T, J = 512, 512, 1024, 512
 FLOPS = 2 * K * N * J * 2
@@ -15,12 +16,14 @@ E5M2 = mybir.dt.float8_e5m2_x4
 E2M1 = mybir.dt.float4_e2m1fn_x4
 COPY = mybir.ActivationFunctionType.Copy
 ADD = mybir.AluOpType.add
+MULT = mybir.AluOpType.mult
 SUBTRACT = mybir.AluOpType.subtract
 
 P = 128
 PACK = 4
 HALF = J // 2
-COLS = T // 2
+CHUNK = 256
+SHARES = ((0, 1), (1, 3), (3, 4))
 
 
 def load_scale_plane(nc, plane, scales):
@@ -37,34 +40,36 @@ def tile_moe_expert_taught_by_page_pl_kernel(
         keep = ctx.enter_context(tc.tile_pool(name="keep", bufs=1))
         psum = ctx.enter_context(tc.psum_pool(name="psum", bufs=1))
 
-        def sb(name, shape, dtype):
-            return keep.tile(shape, dtype, name=name, align_bytes=64)
+        def sb(name, shape, dtype, tag=""):
+            return keep.tile(shape, dtype, name=name, tag=tag, align_bytes=64)
 
         offsets = keep.tile([P, J // 16], U16, name="offsets")
         nc.sync.dma_start(offsets[:], offs)
         half_offsets = [offsets[:, h * (HALF // 16) : (h + 1) * (HALF // 16)] for h in range(2)]
 
-        wn_w = sb("wn_w", [P, 4 * N], U8)
-        wn_s = sb("wn_s", [P, N], U8)
+        wn_w = sb("wn_w", [P, 4 * N], U8, tag="wn_w")
+        wn_s = sb("wn_s", [P, N], U8, tag="wn_s")
         xt_w = sb("xt_w", [P, 2 * T], U8)
         xt_s = sb("xt_s", [P, T], U8)
         wt_w = sb("wt_w", [P, 2 * K], U8)
         wt_s = sb("wt_s", [P, K], U8)
-        for plane in (wn_s, xt_s, wt_s):
-            nc.vector.memset(plane[:].bitcast(I32), 0)
-        nc.sync.dma_start(out=xt_w[:].bitcast(I32), in_=xt_words[0].bitcast(I32))
-        nc.sync.dma_start(out=wn_w[:].bitcast(I32), in_=wn_words[0].rearrange("p n t -> p (n t)").bitcast(I32))
-        load_scale_plane(nc, wn_s, wn_scales)
-        load_scale_plane(nc, xt_s, xt_scales)
-
+        nc.gpsimd.memset(xt_s[:, : T // 2].bitcast(I32), 0)
+        nc.vector.memset(xt_s[:, T // 2 :].bitcast(I32), 0)
+        for plane in (wn_s, wt_s):
+            nc.gpsimd.memset(plane[:].bitcast(I32), 0)
+        us_sb = sb("us_sb", [P, PACK], F32)
+        nc.gpsimd.dma_start(out=us_sb[:], in_=us.rearrange("(p t) o -> p (t o)", t=PACK))
         te_rows = te.rearrange("(p t) c -> p t c", t=PACK)
         run_rows = run.rearrange("(p t) c -> p t c", t=PACK)
         y_rows = out_0.rearrange("(p t) c -> p t c", t=PACK)
         te_sb = [sb("te%d" % t, [P, T], F32) for t in range(PACK)]
-        for t in range(PACK):
+        nc.sync.dma_start(out=xt_w[:].bitcast(I32), in_=xt_words[0].bitcast(I32))
+        nc.sync.dma_start(out=wn_w[:].bitcast(I32), in_=wn_words[0].rearrange("p n t -> p (n t)").bitcast(I32))
+        load_scale_plane(nc, xt_s, xt_scales)
+        nc.sync.dma_start(out=te_sb[0][:], in_=te_rows[:, 0, :])
+        load_scale_plane(nc, wn_s, wn_scales)
+        for t in range(1, PACK):
             nc.sync.dma_start(out=te_sb[t][:], in_=te_rows[:, t, :])
-        us_sb = sb("us_sb", [P, PACK], F32)
-        nc.sync.dma_start(out=us_sb[:], in_=us.rearrange("(p t) o -> p (t o)", t=PACK))
         nc.sync.dma_start(out=wt_w[:].bitcast(I32), in_=wt_words[0].bitcast(I32))
         load_scale_plane(nc, wt_s, wt_scales)
         run_sb = [sb("run%d" % t, [P, T], F32) for t in range(PACK)]
@@ -73,7 +78,11 @@ def tile_moe_expert_taught_by_page_pl_kernel(
 
         pages = [sb("page%d" % t, [P, T], F32) for t in range(PACK)]
         for t in range(PACK):
-            nc.vector.memset(pages[t][:], 0.0)
+            zeroer = nc.vector if t < 2 else nc.gpsimd
+            zeroer.memset(pages[t][:].bitcast(I32), 0)
+
+        identity = sb("identity", [P, P], F32)
+        make_identity(nc, identity[:])
 
         neg_us = sb("neg_us", [P, PACK], F32)
         nc.scalar.activation(out=neg_us[:], in_=us_sb[:], func=COPY, scale=-1.0)
@@ -85,6 +94,7 @@ def tile_moe_expert_taught_by_page_pl_kernel(
 
         for h in range(2):
             nc.vector.tensor_copy(out=xg_w[h][:].bitcast(U16), in_=xt_w[:].bitcast(U16).indirect(half_offsets[h]))
+            nc.vector.tensor_copy(out=xg_s[h][:], in_=xt_s[:].indirect(half_offsets[h]))
         nc.vector.tensor_copy(
             out=wn_wp[:].bitcast(I32).rearrange("p (t c i) -> p c t i", t=PACK, i=4),
             in_=wn_w[:].bitcast(I32).rearrange("p (c i t) -> p c t i", t=PACK, i=4),
@@ -92,13 +102,13 @@ def tile_moe_expert_taught_by_page_pl_kernel(
         nc.vector.tensor_copy(
             out=wn_sp[:].rearrange("p (t m) -> p t m", t=PACK), in_=wn_s[:].rearrange("p (m t) -> p t m", t=PACK)
         )
-        for h in range(2):
-            nc.vector.tensor_copy(out=xg_s[h][:], in_=xt_s[:].indirect(half_offsets[h]))
 
-        p_sb = {}
+        p_bank = {}
+        p_pair = {}
         for h in range(2):
             for u in range(2):
-                bank = psum.tile([P, 2, HALF], F32, name="p_bank%d%d" % (h, u))
+                bank = psum.tile([P, 2, HALF], F32, name="p_bank%d%d" % (h, u), tag="mx%d" % (2 * h + u))
+                p_pair[h, u] = bank
                 for e in range(2):
                     t = 2 * u + e
                     nc.tensor.matmul_mx(
@@ -110,91 +120,138 @@ def tile_moe_expert_taught_by_page_pl_kernel(
                         start=True,
                         stop=True,
                     )
-                p_sb[h, u] = sb("p_sb%d%d" % (h, u), [P, 2, HALF], F32)
-                nc.scalar.copy(out=p_sb[h, u][:], in_=bank[:])
+                    p_bank[h, t] = bank[:, e, :]
 
-        d_codes = sb("d_codes", [P, 4 * J], U8)
-        d_scales = sb("d_scales", [P, J], U8)
-        wt_wp = sb("wt_wp", [P, 2 * K], U8)
-        wt_sp = sb("wt_sp", [P, K], U8)
+        q_banks = [psum.tile([P, J], F32, name="q_bank%d" % t) for t in range(PACK)]
+        q_sb = [sb("q_sb%d" % t, [P, J], F32) for t in range(PACK)]
+        d_planes = [sb("d_planes0", [P, PACK, HALF], BF16, tag="d_planes")]
+
+        te_g = sb("te_g", [P, J], F32, tag="wn_s")
+        nc.vector.tensor_copy(out=te_g[:], in_=te_sb[0][:].indirect(offsets[:]))
+        te_us = sb("te_us", [P, J], F32)
+        nc.gpsimd.tensor_scalar(out=te_us[:], in0=te_g[:], scalar1=us_sb[:, 0:1], scalar2=0.0, op0=MULT, op1=ADD)
+
+        p_sb = {}
         for h in range(2):
-            d_planes = sb("d_planes%d" % h, [P, PACK, HALF], BF16)
-            for t in range(PACK):
-                diff = sb("diff%d%d" % (h, t), [P, HALF], F32)
-                nc.vector.tensor_tensor(
-                    out=diff[:], in0=te_sb[t][:].indirect(half_offsets[h]), in1=p_sb[h, t // 2][:, t % 2, :], op=SUBTRACT
-                )
-                nc.scalar.activation(out=d_planes[:, t, :], in_=diff[:], func=COPY, scale=neg_us[:, t : t + 1])
-            d_grouped = sb("d_grouped%d" % h, [P, HALF, PACK], BF16)
-            dst = d_grouped[:].rearrange("p (c i) t -> p c t i", i=4)
-            src = d_planes[:].rearrange("p t (c i) -> p c t i", i=4)
-            if h == 0:
-                nc.scalar.copy(out=dst, in_=src)
-            else:
-                nc.vector.tensor_copy(
-                    out=wt_wp[:].rearrange("p (t m b) -> p t m b", t=PACK, b=2),
-                    in_=wt_w[:].rearrange("p (m t b) -> p t m b", t=PACK, b=2),
-                )
-                nc.vector.tensor_copy(
-                    out=wt_sp[:].rearrange("p (t m) -> p t m", t=PACK),
-                    in_=wt_s[:].rearrange("p (m t) -> p t m", t=PACK),
-                )
-                nc.vector.tensor_copy(out=dst, in_=src)
-            nc.vector.quantize_mx(
-                out=d_codes[:, 4 * HALF * h : 4 * HALF * (h + 1)].bitcast(E5M2),
-                scales=d_scales[:, HALF * h : HALF * (h + 1)],
-                in_=d_grouped[:].rearrange("p c t -> p (c t)"),
+            single = sb("p_single%d" % h, [P, HALF], F32)
+            nc.scalar.copy(out=single[:], in_=p_bank[h, 1])
+            pair = sb("p_pair%d" % h, [P, 2, HALF], F32, tag="pair%d" % h)
+            nc.scalar.copy(out=pair[:], in_=p_pair[h, 1][:])
+            p_sb[h, 1], p_sb[h, 2], p_sb[h, 3] = single[:], pair[:, 0, :], pair[:, 1, :]
+
+        def first_plane(h):
+            nc.vector.scalar_tensor_tensor(
+                out=d_planes[h][:, 0, :], in0=p_bank[h, 0], scalar=us_sb[:, 0:1], in1=te_us[:, h * HALF : (h + 1) * HALF], op0=MULT, op1=SUBTRACT
             )
 
-        y_pairs = {}
-        y_grouped = [sb("y_grouped%d" % g, [P, COLS, PACK], BF16) for g in range(2)]
-        for u in range(2):
-            for g in range(2):
-                y_pairs[u, g] = sb("y_pairs%d%d" % (u, g), [P, 2, COLS], F32)
+        def plane(h, t, diff):
+            nc.vector.tensor_tensor(
+                out=diff, in0=te_sb[t][:].indirect(half_offsets[h]), in1=p_sb[h, t], op=SUBTRACT
+            )
+            nc.scalar.activation(out=d_planes[h][:, t, :], in_=diff, func=COPY, scale=neg_us[:, t : t + 1])
+
+        def group_views(grouped, planes):
+            return (
+                grouped[:].rearrange("p (c i) t -> p c t i", i=4),
+                planes.rearrange("p t (c i) -> p c t i", i=4),
+            )
+
+        def quantize_d(name, grouped, width):
+            codes = sb("d_codes" + name, [P, 4 * width], U8)
+            scales = sb("d_scales" + name, [P, width], U8)
+            nc.vector.quantize_mx(
+                out=codes[:].bitcast(E5M2), scales=scales[:], in_=grouped[:].rearrange("p c t -> p (c t)")
+            )
+            return codes, scales
+
+        def way_back(b, codes, scales):
+            bank = psum.tile([P, K], F32, name="qt_bank%d" % b, tag="mx%d" % b)
+            nc.tensor.matmul_mx(
+                out=bank[:],
+                lhsT=codes.bitcast(E5M2),
+                lhsT_scale=scales,
+                rhs=wt_w[:].bitcast(E2M1),
+                rhs_scale=wt_s[:],
+                start=True,
+                stop=True,
+            )
+            qt = sb("qt%d" % b, [P, PACK, P], F32)
+            nc.scalar.copy(out=qt[:], in_=bank[:].rearrange("p (m t) -> p t m", t=PACK))
+            for t in range(PACK):
+                nc.tensor.transpose(q_banks[t][:, b * P : (b + 1) * P], qt[:, t, :], identity[:])
+
+        def scatter(t, j0, j1):
+            nc.scalar.copy(out=q_sb[t][:, j0:j1], in_=q_banks[t][:, j0:j1])
+            nc.vector.tensor_copy(out=pages[t][:].indirect(offsets[:, j0 // 16 : j1 // 16]), in_=q_sb[t][:, j0:j1])
+
+        first_plane(0)
+        for t in range(1, PACK):
+            plane(0, t, sb("diff0%d" % t, [P, HALF], F32)[:])
+        grouped = []
+        for b in range(2):
+            grouped.append(sb("d_grouped%d" % b, [P, P, PACK], BF16, tag="grouped%d" % b))
+            dst, src = group_views(grouped[b], d_planes[0][:, :, b * P : (b + 1) * P])
+            nc.scalar.copy(out=dst, in_=src)
+        d_planes.append(sb("d_planes1", [P, PACK, HALF], BF16, tag="d_planes"))
+        diff_pair = sb("diff_pair", [P, 2, HALF], F32, tag="pair0")
+        plane(1, 1, diff_pair[:, 0, :])
+        plane(1, 2, diff_pair[:, 1, :])
+        codes, scales = quantize_d("0", grouped[0], P)
+        way_back(0, codes[:], scales[:])
+        plane(1, 3, sb("diff13", [P, HALF], F32, tag="grouped0")[:])
+        first_plane(1)
+        codes1, scales1 = quantize_d("1", grouped[1], P)
+        grouped_rest = sb("d_grouped_rest", [P, HALF, PACK], BF16)
+        dst, src = group_views(grouped_rest, d_planes[1][:])
+        nc.vector.tensor_copy(out=dst, in_=src)
+        codes2, scales2 = quantize_d("2", grouped_rest, HALF)
+        for t in range(2):
+            scatter(t, 0, P)
+        way_back(1, codes1[:], scales1[:])
+        for t in range(2):
+            scatter(t, P, HALF)
+        for b in range(2):
+            way_back(2 + b, codes2[:, 4 * P * b : 4 * P * (b + 1)], scales2[:, P * b : P * (b + 1)])
+
+        y_pairs = [sb("y_pairs%d" % u, [P, 2 * T], F32) for u in range(2)]
+        y_views = [y_pairs[u][:].rearrange("p (g e c) -> p g e c", e=2, c=CHUNK) for u in range(2)]
+        y_grouped = [sb("y_grouped%d" % s, [P, (g1 - g0) * CHUNK, PACK], BF16) for s, (g0, g1) in enumerate(SHARES)]
         y_codes = sb("y_codes", [P, 4 * T], U8)
         y_scales = sb("y_scales", [P, T], U8)
         words_out = out_1[0].rearrange("p c r -> p (c r)").bitcast(I32)
         scales_out = out_2[0].bitcast(I32)
 
         for t in range(PACK):
-            bank = psum.tile([P, J], F32, name="q_bank%d" % t)
-            nc.tensor.matmul_mx(
-                out=bank[:],
-                lhsT=wt_wp[:, 2 * P * t : 2 * P * (t + 1)].bitcast(E2M1),
-                lhsT_scale=wt_sp[:, P * t : P * (t + 1)],
-                rhs=d_codes[:].bitcast(E5M2),
-                rhs_scale=d_scales[:],
-                start=True,
-                stop=True,
-            )
-            q_sb = sb("q_sb%d" % t, [P, J], F32)
-            nc.scalar.copy(out=q_sb[:], in_=bank[:])
-            nc.vector.tensor_copy(out=pages[t][:].indirect(offsets[:]), in_=q_sb[:])
+            scatter(t, HALF if t < 2 else 0, J)
             u, e = divmod(t, 2)
             last = t == PACK - 1
-            for g in range(2):
-                cols = slice(g * COLS, (g + 1) * COLS)
-                adder = nc.vector if last else nc.gpsimd
-                adder.tensor_tensor(out=y_pairs[u, g][:, e, :], in0=pages[t][:, cols], in1=run_sb[t][:, cols], op=ADD)
-                nc.sync.dma_start(out=y_rows[:, t, cols], in_=y_pairs[u, g][:, e, :])
+            page = pages[t][:].rearrange("p (g c) -> p g c", c=CHUNK)
+            old = run_sb[t][:].rearrange("p (g c) -> p g c", c=CHUNK)
+            if last:
+                for g0, g1 in SHARES:
+                    nc.vector.tensor_tensor(out=y_views[u][:, g0:g1, e, :], in0=page[:, g0:g1, :], in1=old[:, g0:g1, :], op=ADD)
+            else:
+                nc.gpsimd.tensor_tensor(out=y_views[u][:, :, e, :], in0=page, in1=old, op=ADD)
+            nc.sync.dma_start(out=y_rows[:, t, :].rearrange("p (g c) -> p g c", c=CHUNK), in_=y_views[u][:, :, e, :])
             if e == 1:
-                for g in range(2):
-                    dst = y_grouped[g][:, :, 2 * u : 2 * u + 2]
-                    src = y_pairs[u, g][:].rearrange("p e c -> p c e")
-                    if last and g == 1:
+                for s, (g0, g1) in enumerate(SHARES):
+                    dst = y_grouped[s][:, :, 2 * u : 2 * u + 2].rearrange("p (g c) e -> p g c e", c=CHUNK)
+                    src = y_views[u][:, g0:g1, :, :].rearrange("p g e c -> p g c e")
+                    if last and s == 1:
                         nc.vector.tensor_copy(out=dst, in_=src)
                     else:
                         nc.scalar.copy(out=dst, in_=src)
 
-        for g in (1, 0):
+        for s, (g0, g1) in enumerate(SHARES):
+            c0, c1 = g0 * CHUNK, g1 * CHUNK
             nc.vector.quantize_mx(
-                out=y_codes[:, 4 * COLS * g : 4 * COLS * (g + 1)].bitcast(E4M3),
-                scales=y_scales[:, COLS * g : COLS * (g + 1)],
-                in_=y_grouped[g][:].rearrange("p c t -> p (c t)"),
+                out=y_codes[:, 4 * c0 : 4 * c1].bitcast(E4M3),
+                scales=y_scales[:, c0:c1],
+                in_=y_grouped[s][:].rearrange("p c t -> p (c t)"),
             )
-            nc.sync.dma_start(
-                out=words_out[:, COLS * g : COLS * (g + 1)], in_=y_codes[:].bitcast(I32)[:, COLS * g : COLS * (g + 1)]
-            )
+            if s > 0:
+                w0 = 0 if s == 1 else c0
+                nc.sync.dma_start(out=words_out[:, w0:c1], in_=y_codes[:].bitcast(I32)[:, w0:c1])
         for q in range(4):
             queue = nc.sync if q % 2 == 0 else nc.scalar
             queue.dma_start(out=scales_out[4 * q : 4 * q + 4, :], in_=y_scales[32 * q : 32 * q + 4, :].bitcast(I32))

@@ -129,7 +129,7 @@ def tile_moe_expert_taught_by_page_pl_kernel(
         te_g = sb("te_g", [P, J], F32, tag="wn_s")
         nc.vector.tensor_copy(out=te_g[:], in_=te_sb[0][:].indirect(offsets[:]))
         te_us = sb("te_us", [P, J], F32)
-        nc.gpsimd.tensor_scalar(out=te_us[:], in0=te_g[:], scalar1=us_sb[:, 0:1], scalar2=0.0, op0=MULT, op1=ADD)
+        nc.vector.tensor_scalar(out=te_us[:], in0=te_g[:], scalar1=us_sb[:, 0:1], scalar2=None, op0=MULT)
 
         p_sb = {}
         for h in range(2):
@@ -227,11 +227,9 @@ def tile_moe_expert_taught_by_page_pl_kernel(
             last = t == PACK - 1
             page = pages[t][:].rearrange("p (g c) -> p g c", c=CHUNK)
             old = run_sb[t][:].rearrange("p (g c) -> p g c", c=CHUNK)
-            if last:
-                for g0, g1 in SHARES:
-                    nc.vector.tensor_tensor(out=y_views[u][:, g0:g1, e, :], in0=page[:, g0:g1, :], in1=old[:, g0:g1, :], op=ADD)
-            else:
-                nc.gpsimd.tensor_tensor(out=y_views[u][:, :, e, :], in0=page, in1=old, op=ADD)
+            adder = nc.vector if last else nc.gpsimd
+            for g0, g1 in SHARES if e == 1 else ((0, T // CHUNK),):
+                adder.tensor_tensor(out=y_views[u][:, g0:g1, e, :], in0=page[:, g0:g1, :], in1=old[:, g0:g1, :], op=ADD)
             nc.sync.dma_start(out=y_rows[:, t, :].rearrange("p (g c) -> p g c", c=CHUNK), in_=y_views[u][:, :, e, :])
             if e == 1:
                 for s, (g0, g1) in enumerate(SHARES):
@@ -249,9 +247,7 @@ def tile_moe_expert_taught_by_page_pl_kernel(
                 scales=y_scales[:, c0:c1],
                 in_=y_grouped[s][:].rearrange("p c t -> p (c t)"),
             )
-            if s > 0:
-                w0 = 0 if s == 1 else c0
-                nc.sync.dma_start(out=words_out[:, w0:c1], in_=y_codes[:].bitcast(I32)[:, w0:c1])
+            nc.sync.dma_start(out=words_out[:, c0:c1], in_=y_codes[:].bitcast(I32)[:, c0:c1])
         for q in range(4):
             queue = nc.sync if q % 2 == 0 else nc.scalar
             queue.dma_start(out=scales_out[4 * q : 4 * q + 4, :], in_=y_scales[32 * q : 32 * q + 4, :].bitcast(I32))

from contextlib import ExitStack

import concourse.mybir as mybir
from concourse.masks import make_identity

K, N, T, J = 512, 512, 1024, 512
FLOPS = 2 * K * N * J * 2

F32 = mybir.dt.float32
BF16 = mybir.dt.bfloat16
I32 = mybir.dt.int32
U16 = mybir.dt.uint16
U8 = mybir.dt.uint8
E4M3 = mybir.dt.float8_e4m3fn_x4
E5M2 = mybir.dt.float8_e5m2_x4
E2M1 = mybir.dt.float4_e2m1fn_x4
COPY = mybir.ActivationFunctionType.Copy
ADD = mybir.AluOpType.add
MULT = mybir.AluOpType.mult
SUBTRACT = mybir.AluOpType.subtract

P = 128
PACK = 4
HALF = J // 2
CHUNK = 256
SHARES = ((0, 1), (1, 3), (3, 4))


def load_scale_plane(nc, plane, scales):
    words = scales[0].bitcast(I32)
    for q in range(4):
        nc.sync.dma_start(out=plane[32 * q : 32 * q + 4, :].bitcast(I32), in_=words[4 * q : 4 * q + 4, :])


def tile_moe_expert_taught_by_page_pl_kernel(
    tc, xt_words, xt_scales, wn_words, wn_scales, te, us, wt_words, wt_scales, run, offs, out_0, out_1, out_2
):
    nc = tc.nc
    with ExitStack() as ctx:
        keep = ctx.enter_context(tc.tile_pool(name="keep", bufs=1))
        psum = ctx.enter_context(tc.psum_pool(name="psum", bufs=1))

        def sb(name, shape, dtype, tag=""):
            return keep.tile(shape, dtype, name=name, tag=tag, align_bytes=64)

        offsets = keep.tile([P, J // 16], U16, name="offsets")
        nc.sync.dma_start(offsets[:], offs)
        half_offsets = [offsets[:, h * (HALF // 16) : (h + 1) * (HALF // 16)] for h in range(2)]

        wn_w = sb("wn_w", [P, 4 * N], U8, tag="wn_w")
        wn_s = sb("wn_s", [P, N], U8, tag="wn_s")
        xt_w = sb("xt_w", [P, 2 * T], U8)
        xt_s = sb("xt_s", [P, T], U8)
        wt_w = sb("wt_w", [P, 2 * K], U8)
        wt_s = sb("wt_s", [P, K], U8)
        nc.gpsimd.memset(xt_s[:, : T // 2].bitcast(I32), 0)
        nc.vector.memset(xt_s[:, T // 2 :].bitcast(I32), 0)
        for plane in (wn_s, wt_s):
            nc.gpsimd.memset(plane[:].bitcast(I32), 0)
        us_sb = sb("us_sb", [P, PACK], F32)
        nc.gpsimd.dma_start(out=us_sb[:], in_=us.rearrange("(p t) o -> p (t o)", t=PACK))
        te_rows = te.rearrange("(p t) c -> p t c", t=PACK)
        run_rows = run.rearrange("(p t) c -> p t c", t=PACK)
        y_rows = out_0.rearrange("(p t) c -> p t c", t=PACK)
        te_sb = [sb("te%d" % t, [P, T], F32) for t in range(PACK)]
        nc.sync.dma_start(out=xt_w[:].bitcast(I32), in_=xt_words[0].bitcast(I32))
        nc.sync.dma_start(out=wn_w[:].bitcast(I32), in_=wn_words[0].rearrange("p n t -> p (n t)").bitcast(I32))
        load_scale_plane(nc, xt_s, xt_scales)
        nc.sync.dma_start(out=te_sb[0][:], in_=te_rows[:, 0, :])
        load_scale_plane(nc, wn_s, wn_scales)
        for t in range(1, PACK):
            nc.sync.dma_start(out=te_sb[t][:], in_=te_rows[:, t, :])
        nc.sync.dma_start(out=wt_w[:].bitcast(I32), in_=wt_words[0].bitcast(I32))
        load_scale_plane(nc, wt_s, wt_scales)
        run_sb = [sb("run%d" % t, [P, T], F32) for t in range(PACK)]
        for t in range(PACK):
            nc.sync.dma_start(out=run_sb[t][:], in_=run_rows[:, t, :])

        pages = [sb("page%d" % t, [P, T], F32) for t in range(PACK)]
        for t in range(PACK):
            zeroer = nc.vector if t < 2 else nc.gpsimd
            zeroer.memset(pages[t][:].bitcast(I32), 0)

        identity = sb("identity", [P, P], F32)
        make_identity(nc, identity[:])

        neg_us = sb("neg_us", [P, PACK], F32)
        nc.scalar.activation(out=neg_us[:], in_=us_sb[:], func=COPY, scale=-1.0)

        xg_w = [sb("xg_w%d" % h, [P, 2 * HALF], U8) for h in range(2)]
        xg_s = [sb("xg_s%d" % h, [P, HALF], U8) for h in range(2)]
        wn_wp = sb("wn_wp", [P, 4 * N], U8)
        wn_sp = sb("wn_sp", [P, N], U8)

        for h in range(2):
            nc.vector.tensor_copy(out=xg_w[h][:].bitcast(U16), in_=xt_w[:].bitcast(U16).indirect(half_offsets[h]))
            nc.vector.tensor_copy(out=xg_s[h][:], in_=xt_s[:].indirect(half_offsets[h]))
        nc.vector.tensor_copy(
            out=wn_wp[:].bitcast(I32).rearrange("p (t c i) -> p c t i", t=PACK, i=4),
            in_=wn_w[:].bitcast(I32).rearrange("p (c i t) -> p c t i", t=PACK, i=4),
        )
        nc.vector.tensor_copy(
            out=wn_sp[:].rearrange("p (t m) -> p t m", t=PACK), in_=wn_s[:].rearrange("p (m t) -> p t m", t=PACK)
        )

        p_bank = {}
        p_pair = {}
        for h in range(2):
            for u in range(2):
                bank = psum.tile([P, 2, HALF], F32, name="p_bank%d%d" % (h, u), tag="mx%d" % (2 * h + u))
                p_pair[h, u] = bank
                for e in range(2):
                    t = 2 * u + e
                    nc.tensor.matmul_mx(
                        out=bank[:, e, :],
                        lhsT=wn_wp[:, 4 * P * t : 4 * P * (t + 1)].bitcast(E4M3),
                        lhsT_scale=wn_sp[:, P * t : P * (t + 1)],
                        rhs=xg_w[h][:].bitcast(E2M1),
                        rhs_scale=xg_s[h][:],
                        start=True,
                        stop=True,
                    )
                    p_bank[h, t] = bank[:, e, :]

        q_banks = [psum.tile([P, J], F32, name="q_bank%d" % t) for t in range(PACK)]
        q_sb = [sb("q_sb%d" % t, [P, J], F32) for t in range(PACK)]
        d_planes = [sb("d_planes0", [P, PACK, HALF], BF16, tag="d_planes")]

        te_g = sb("te_g", [P, J], F32, tag="wn_s")
        nc.vector.tensor_copy(out=te_g[:], in_=te_sb[0][:].indirect(offsets[:]))
        te_us = sb("te_us", [P, J], F32)
        nc.vector.tensor_scalar(out=te_us[:], in0=te_g[:], scalar1=us_sb[:, 0:1], scalar2=None, op0=MULT)

        p_sb = {}
        for h in range(2):
            single = sb("p_single%d" % h, [P, HALF], F32)
            nc.scalar.copy(out=single[:], in_=p_bank[h, 1])
            pair = sb("p_pair%d" % h, [P, 2, HALF], F32, tag="pair%d" % h)
            nc.scalar.copy(out=pair[:], in_=p_pair[h, 1][:])
            p_sb[h, 1], p_sb[h, 2], p_sb[h, 3] = single[:], pair[:, 0, :], pair[:, 1, :]

        def first_plane(h):
            nc.vector.scalar_tensor_tensor(
                out=d_planes[h][:, 0, :], in0=p_bank[h, 0], scalar=us_sb[:, 0:1], in1=te_us[:, h * HALF : (h + 1) * HALF], op0=MULT, op1=SUBTRACT
            )

        def plane(h, t, diff):
            nc.vector.tensor_tensor(
                out=diff, in0=te_sb[t][:].indirect(half_offsets[h]), in1=p_sb[h, t], op=SUBTRACT
            )
            nc.scalar.activation(out=d_planes[h][:, t, :], in_=diff, func=COPY, scale=neg_us[:, t : t + 1])

        def group_views(grouped, planes):
            return (
                grouped[:].rearrange("p (c i) t -> p c t i", i=4),
                planes.rearrange("p t (c i) -> p c t i", i=4),
            )

        def quantize_d(name, grouped, width):
            codes = sb("d_codes" + name, [P, 4 * width], U8)
            scales = sb("d_scales" + name, [P, width], U8)
            nc.vector.quantize_mx(
                out=codes[:].bitcast(E5M2), scales=scales[:], in_=grouped[:].rearrange("p c t -> p (c t)")
            )
            return codes, scales

        def way_back(b, codes, scales):
            bank = psum.tile([P, K], F32, name="qt_bank%d" % b, tag="mx%d" % b)
            nc.tensor.matmul_mx(
                out=bank[:],
                lhsT=codes.bitcast(E5M2),
                lhsT_scale=scales,
                rhs=wt_w[:].bitcast(E2M1),
                rhs_scale=wt_s[:],
                start=True,
                stop=True,
            )
            qt = sb("qt%d" % b, [P, PACK, P], F32)
            nc.scalar.copy(out=qt[:], in_=bank[:].rearrange("p (m t) -> p t m", t=PACK))
            for t in range(PACK):
                nc.tensor.transpose(q_banks[t][:, b * P : (b + 1) * P], qt[:, t, :], identity[:])

        def scatter(t, j0, j1):
            nc.scalar.copy(out=q_sb[t][:, j0:j1], in_=q_banks[t][:, j0:j1])
            nc.vector.tensor_copy(out=pages[t][:].indirect(offsets[:, j0 // 16 : j1 // 16]), in_=q_sb[t][:, j0:j1])

        first_plane(0)
        for t in range(1, PACK):
            plane(0, t, sb("diff0%d" % t, [P, HALF], F32)[:])
        grouped = []
        for b in range(2):
            grouped.append(sb("d_grouped%d" % b, [P, P, PACK], BF16, tag="grouped%d" % b))
            dst, src = group_views(grouped[b], d_planes[0][:, :, b * P : (b + 1) * P])
            nc.scalar.copy(out=dst, in_=src)
        d_planes.append(sb("d_planes1", [P, PACK, HALF], BF16, tag="d_planes"))
        diff_pair = sb("diff_pair", [P, 2, HALF], F32, tag="pair0")
        plane(1, 1, diff_pair[:, 0, :])
        plane(1, 2, diff_pair[:, 1, :])
        codes, scales = quantize_d("0", grouped[0], P)
        way_back(0, codes[:], scales[:])
        plane(1, 3, sb("diff13", [P, HALF], F32, tag="grouped0")[:])
        first_plane(1)
        codes1, scales1 = quantize_d("1", grouped[1], P)
        grouped_rest = sb("d_grouped_rest", [P, HALF, PACK], BF16)
        dst, src = group_views(grouped_rest, d_planes[1][:])
        nc.vector.tensor_copy(out=dst, in_=src)
        codes2, scales2 = quantize_d("2", grouped_rest, HALF)
        for t in range(2):
            scatter(t, 0, P)
        way_back(1, codes1[:], scales1[:])
        for t in range(2):
            scatter(t, P, HALF)
        for b in range(2):
            way_back(2 + b, codes2[:, 4 * P * b : 4 * P * (b + 1)], scales2[:, P * b : P * (b + 1)])

        y_pairs = [sb("y_pairs%d" % u, [P, 2 * T], F32) for u in range(2)]
        y_views = [y_pairs[u][:].rearrange("p (g e c) -> p g e c", e=2, c=CHUNK) for u in range(2)]
        y_grouped = [sb("y_grouped%d" % s, [P, (g1 - g0) * CHUNK, PACK], BF16) for s, (g0, g1) in enumerate(SHARES)]
        y_codes = sb("y_codes", [P, 4 * T], U8)
        y_scales = sb("y_scales", [P, T], U8)
        words_out = out_1[0].rearrange("p c r -> p (c r)").bitcast(I32)
        scales_out = out_2[0].bitcast(I32)

        for t in range(PACK):
            scatter(t, HALF if t < 2 else 0, J)
            u, e = divmod(t, 2)
            last = t == PACK - 1
            page = pages[t][:].rearrange("p (g c) -> p g c", c=CHUNK)
            old = run_sb[t][:].rearrange("p (g c) -> p g c", c=CHUNK)
            adder = nc.vector if last else nc.gpsimd
            for g0, g1 in SHARES if e == 1 else ((0, T // CHUNK),):
                adder.tensor_tensor(out=y_views[u][:, g0:g1, e, :], in0=page[:, g0:g1, :], in1=old[:, g0:g1, :], op=ADD)
            nc.sync.dma_start(out=y_rows[:, t, :].rearrange("p (g c) -> p g c", c=CHUNK), in_=y_views[u][:, :, e, :])
            if e == 1:
                for s, (g0, g1) in enumerate(SHARES):
                    dst = y_grouped[s][:, :, 2 * u : 2 * u + 2].rearrange("p (g c) e -> p g c e", c=CHUNK)
                    src = y_views[u][:, g0:g1, :, :].rearrange("p g e c -> p g c e")
                    if last and s == 1:
                        nc.vector.tensor_copy(out=dst, in_=src)
                    else:
                        nc.scalar.copy(out=dst, in_=src)

        for s, (g0, g1) in enumerate(SHARES):
            c0, c1 = g0 * CHUNK, g1 * CHUNK
            nc.vector.quantize_mx(
                out=y_codes[:, 4 * c0 : 4 * c1].bitcast(E4M3),
                scales=y_scales[:, c0:c1],
                in_=y_grouped[s][:].rearrange("p c t -> p (c t)"),
            )
            nc.sync.dma_start(out=words_out[:, c0:c1], in_=y_codes[:].bitcast(I32)[:, c0:c1])
        for q in range(4):
            queue = nc.sync if q % 2 == 0 else nc.scalar
            queue.dma_start(out=scales_out[4 * q : 4 * q + 4, :], in_=y_scales[32 * q : 32 * q + 4, :].bitcast(I32))
